import numpy as np
import ml_dtypes


def mxq(x, axis, fmt="e4m3"):
    dtype, down = {"e4m3": (ml_dtypes.float8_e4m3fn, 7), "e5m2": (ml_dtypes.float8_e5m2, 14)}[fmt]
    v = np.moveaxis(np.asarray(x, np.float32).astype(ml_dtypes.bfloat16).astype(np.float64), axis, -1)
    blocks = v.reshape(v.shape[:-1] + (-1, 32))
    amax = np.abs(blocks).max(-1, keepdims=True)
    byte = np.maximum(np.where(amax > 0, np.frexp(amax)[1] - 1 + 127, 0) - down, 1)
    scale = np.exp2(byte - 127.0)
    codes = (blocks / scale).astype(np.float32).astype(dtype).astype(np.float64)
    return np.moveaxis((codes * scale).reshape(v.shape), -1, axis)


WIDE = False


def mx_kscale(k):
    if not WIDE:
        return np.ones(k)
    levels = np.array([10, -10, 5, -5, 0])
    if k % 512:
        return np.exp2(np.random.permutation(np.resize(levels, k // 32))).repeat(32)
    a = np.empty((k // 512, 16))
    for p in range(k // 512):
        a[p, :8] = np.random.permutation(np.resize(levels, 8))
        for g in range(8):
            far = levels[np.abs(levels - a[p, g]) >= 10]
            a[p, g + 8] = far[np.random.randint(len(far))]
    return np.exp2(a.ravel()).repeat(32)


BF16 = ml_dtypes.bfloat16


def bf(x):
    return np.asarray(x, np.float32).astype(BF16)


def f64(x):
    return np.asarray(x).astype(np.float64)


E2M1 = np.array([0.0, 0.5, 1.0, 1.5, 2.0, 3.0, 4.0, 6.0, -0.0, -0.5, -1.0, -1.5, -2.0, -3.0, -4.0, -6.0])


def pack_weight(w, fmt):
    k, n = w.shape
    w = f64(bf(w)).reshape(k // 32, 32, n)
    amax = np.abs(w).max(1)
    if fmt == "e4m3":
        byte = np.frexp(amax)[1] - 1 + 127 - 7
    else:
        mant, ex = np.frexp(amax / 6.0)
        byte = np.where(mant > 0.5, ex, ex - 1) + 127
    byte = np.clip(np.where(amax > 0, byte, 1), 1, 254)
    scaled = (w * np.exp2(127.0 - byte)[:, None, :]).reshape(k, n).astype(np.float32)
    by_word = np.ascontiguousarray(scaled.reshape(k // 512, 128, 4, n).transpose(0, 1, 3, 2))
    if fmt == "e4m3":
        words = by_word.astype(ml_dtypes.float8_e4m3fn).view(np.uint8)
    else:
        c = by_word.astype(ml_dtypes.float4_e2m1fn).view(np.uint8) & 0xF
        words = c[..., 0::2] | (c[..., 1::2] << 4)
    return np.ascontiguousarray(words), np.ascontiguousarray(byte.astype(np.uint8).reshape(k // 512, 16, n))


def unpack_weight(words, scales, fmt):
    g, p, n, _ = words.shape
    if fmt == "e4m3":
        vals = np.ascontiguousarray(words).view(ml_dtypes.float8_e4m3fn).astype(np.float64)
    else:
        nib = np.empty((g, p, n, 4), np.uint8)
        nib[..., 0::2] = words & 0xF
        nib[..., 1::2] = words >> 4
        vals = E2M1[nib]
    vals = vals * np.repeat(np.exp2(scales.astype(np.float64) - 127.0), 8, axis=1)[..., None]
    return vals.transpose(0, 1, 3, 2).reshape(g * 512, n)
def pack4(w):
    words, scales = pack_weight(w, "e2m1")
    return words.reshape(words.shape[0], 128, -1), scales


def unpack4(words, scales):
    return unpack_weight(words.reshape(words.shape[0], 128, -1, 2), scales, "e2m1")


E, R, K, M, N = 512, 4, 512, 1024, 1536
P = E * R


def setup_inputs():
    s = mx_kscale(K)
    t = mx_kscale(P)
    tm = t.reshape(E, R)[:, 0]
    right = np.random.standard_normal((P, N)) / np.sqrt(P) / t[:, None]
    right_words, right_scales = pack4(right)
    return {"z": bf(np.random.standard_normal((P, K)) * s),
            "c": bf(np.random.standard_normal((K, M)) / np.sqrt(K) / s[:, None]),
            "fitness": bf(np.random.standard_normal(E) * tm),
            "right_words": right_words,
            "right_scales": right_scales,
            "eta": bf(1 + 0.1 * np.random.standard_normal(M)),
            "theta": bf(0.5 * np.random.standard_normal((M, N)))}


def reference(z, c, fitness, right_words, right_scales, eta, theta):
    left = mxq(f64(z), 1, "e4m3") @ mxq(f64(c), 0, "e4m3")
    h = (left.reshape(E, R, M) * f64(fitness)[:, None, None]).reshape(P, M)
    b = unpack4(right_words, right_scales)
    g = mxq(h, 0, "e4m3").T @ b
    return f64(theta) + f64(eta)[:, None] * g

@@ -1,0 +1,296 @@
+from contextlib import ExitStack
+
+import concourse.mybir as mybir
+from concourse.masks import make_identity
+
+POP, K, M, N = 2048, 512, 1024, 1536
+FLOPS = 2 * POP * K * M + 2 * POP * M * N
+
+F32 = mybir.dt.float32
+BF16 = mybir.dt.bfloat16
+I32 = mybir.dt.int32
+U32 = mybir.dt.uint32
+U8 = mybir.dt.uint8
+FP8X4 = mybir.dt.float8_e4m3fn_x4
+FP4X4 = mybir.dt.float4_e2m1fn_x4
+COPY = mybir.ActivationFunctionType.Copy
+MULT = mybir.AluOpType.mult
+ADD = mybir.AluOpType.add
+
+P = 128
+PACK = 4
+GROUPS = POP // (P * PACK)
+M_TILES = M // P
+N_TILE = 512
+N_TILES = N // N_TILE
+BANKS = 8
+
+
+def tile_low_rank_es_update_s13_kernel(tc, z, c, fitness, right_words, right_scales, eta, theta, out):
+    nc = tc.nc
+    with ExitStack() as ctx:
+        keep = ctx.enter_context(tc.tile_pool(name="keep", bufs=1))
+        psum = ctx.enter_context(tc.psum_pool(name="psum", bufs=1))
+        ctx.enter_context(tc.manual_schedule())
+
+        def sb(name, shape, dtype):
+            return keep.tile(shape, dtype, name=name, align_bytes=64)
+
+        free_banks = list(range(BANKS))
+
+        def take_bank(dtype=F32, width=512):
+            b = free_banks[0]
+            free_banks.remove(b)
+            t = psum.tile([P, width], dtype, name="bank%d" % b)
+            return b, t
+
+        ident = sb("ident", [P, P], F32)
+        ident_bf = sb("ident_bf", [P, P], BF16)
+        vec_rows = sb("vec_rows", [P, P], BF16)
+        coef = sb("coef", [P, 16], F32)
+        warm = sb("warm", [P, 8], F32)
+
+        z_raw = [sb("z_raw%d" % g, [P, PACK, K], BF16) for g in range(GROUPS)]
+        z_grp = [sb("z_grp%d" % g, [P, PACK, P, PACK], BF16) for g in range(GROUPS)]
+        z_codes = [sb("z_codes%d" % g, [P, PACK * P], U32) for g in range(GROUPS)]
+        z_scales = [sb("z_scales%d" % g, [P, PACK * P], U8) for g in range(GROUPS)]
+        c_chunks = [(0, 256), (256, 512), (512, 1024)]
+        c_raw = [sb("c_raw%d" % i, [P, PACK, hi - lo], BF16) for i, (lo, hi) in enumerate(c_chunks)]
+        c_grp = sb("c_grp", [P, M, PACK], BF16)
+        c_codes = sb("c_codes", [P, M], U32)
+        c_scales = sb("c_scales", [P, M], U8)
+        h_grp = [sb("h_grp%d" % g, [P, M, PACK], BF16) for g in range(GROUPS)]
+        h_codes = [sb("h_codes%d" % g, [P, M], U32) for g in range(GROUPS)]
+        h_scales = [sb("h_scales%d" % g, [P, M], U8) for g in range(GROUPS)]
+        b_words = [sb("b_words%d" % n, [P, GROUPS, 2 * N_TILE], U8) for n in range(N_TILES)]
+        b_scales = [sb("b_scales%d" % n, [P, GROUPS, N_TILE], U8) for n in range(N_TILES)]
+        theta_sb = [sb("theta%d" % j, [P, 2, N], BF16) for j in range(M_TILES // 2)]
+
+        def load_z(g, t0, t1):
+            rows = z[g * 512 : (g + 1) * 512, :].rearrange("(p t) k -> p t k", t=PACK)
+            nc.sync.dma_start(out=z_raw[g][:, t0:t1, :], in_=rows[:, t0:t1, :])
+
+        def load_c(i):
+            lo, hi = c_chunks[i]
+            nc.sync.dma_start(out=c_raw[i][:], in_=c.rearrange("(p j) w -> p j w", j=PACK)[:, :, lo:hi])
+
+        def load_b(n):
+            rows = right_scales.bitcast(I32).rearrange("g (q r) w -> r q g w", r=4)
+            for r in range(4):
+                nc.sync.dma_start(
+                    out=b_scales[n][:].bitcast(I32)[r:P:32, :, :],
+                    in_=rows[r, :, :, n * 128 : (n + 1) * 128],
+                )
+            words = right_words.bitcast(I32).rearrange("g p w -> p g w")
+            nc.sync.dma_start(out=b_words[n][:].bitcast(I32), in_=words[:, :, n * 256 : (n + 1) * 256])
+
+        def load_theta(j):
+            nc.sync.dma_start(
+                out=theta_sb[j][:], in_=theta[j * 256 : (j + 1) * 256, :].rearrange("(a p) n -> p a n", p=P)
+            )
+
+        def transpose_z(g, half):
+            b, bank = take_bank()
+            for tt in range(2):
+                words = z_raw[g][:, 2 * half + tt, :].bitcast(F32)
+                for u in range(2):
+                    col = (2 * tt + u) * P
+                    nc.tensor.transpose(bank[:, col : col + P], words[:, u : 2 * P : 2], ident[:])
+            return b, bank
+
+        def copy_z(g, half, held, on_scalar):
+            b, bank = held
+            dst = z_grp[g][:, 2 * half : 2 * half + 2, :, :].bitcast(F32)
+            src = bank[:].rearrange("p (t u r) -> p t r u", t=2, u=2)
+            if on_scalar:
+                nc.scalar.copy(out=dst, in_=src)
+            else:
+                nc.vector.tensor_copy(out=dst, in_=src)
+            free_banks.append(b)
+
+        def quantize_z(g, half):
+            cols = slice(half * 256, (half + 1) * 256)
+            nc.vector.quantize_mx(
+                out=z_codes[g][:, cols].bitcast(FP8X4),
+                scales=z_scales[g][:, cols],
+                in_=z_grp[g][:, 2 * half : 2 * half + 2, :, :].rearrange("p t r j -> p (t r j)"),
+            )
+
+        def group_c(i, lo, hi):
+            base = c_chunks[i][0]
+            nc.vector.tensor_copy(
+                out=c_grp[:, lo:hi, :].rearrange("p (c i) t -> p c t i", i=4),
+                in_=c_raw[i][:, :, lo - base : hi - base].rearrange("p t (c i) -> p c t i", i=4),
+            )
+
+        def quantize_c(lo, hi):
+            nc.vector.quantize_mx(
+                out=c_codes[:, lo:hi].bitcast(FP8X4),
+                scales=c_scales[:, lo:hi],
+                in_=c_grp[:, lo:hi, :].rearrange("p w j -> p (w j)"),
+            )
+
+        def first_product(g, m, on_scalar=True):
+            b, bank = take_bank()
+            cols = slice(m * P, (m + 1) * P)
+            for t in range(PACK):
+                rows = slice(t * P, (t + 1) * P)
+                nc.tensor.matmul_mx(
+                    out=bank[:, rows],
+                    lhsT=z_codes[g][:, rows].bitcast(FP8X4),
+                    lhsT_scale=z_scales[g][:, rows],
+                    rhs=c_codes[:, cols].bitcast(FP8X4),
+                    rhs_scale=c_scales[:, cols],
+                    start=True,
+                    stop=True,
+                )
+            src = bank[:].rearrange("p (t w) -> p w t", t=PACK)
+            if on_scalar:
+                nc.scalar.activation(out=h_grp[g][:, cols, :], in_=src, func=COPY, scale=coef[:, g : g + 1])
+            else:
+                nc.vector.tensor_scalar(
+                    out=h_grp[g][:, cols, :], in0=src, scalar1=coef[:, g : g + 1], scalar2=None, op0=MULT
+                )
+            free_banks.append(b)
+
+        def quantize_h(g, m0, m1):
+            cols = slice(m0 * P, m1 * P)
+            nc.vector.quantize_mx(
+                out=h_codes[g][:, cols].bitcast(FP8X4),
+                scales=h_scales[g][:, cols],
+                in_=h_grp[g][:, cols, :].rearrange("p w j -> p (w j)"),
+            )
+
+        def second_pass(bank, g, m, n, lo, hi):
+            cols = slice(m * P, (m + 1) * P)
+            nc.tensor.matmul_mx(
+                out=bank[:, 0 : hi - lo],
+                lhsT=h_codes[g][:, cols].bitcast(FP8X4),
+                lhsT_scale=h_scales[g][:, cols],
+                rhs=b_words[n][:, g, 2 * lo : 2 * hi].bitcast(FP4X4),
+                rhs_scale=b_scales[n][:, g, lo:hi],
+                start=(g == 0),
+                stop=(g == GROUPS - 1),
+            )
+
+        def finish(held, m, n, lo, hi):
+            b, bank = held
+            result = sb("result_%d_%d_%d" % (m, n, lo), [P, hi - lo], F32)
+            cols = slice(n * N_TILE + lo, n * N_TILE + hi)
+            nc.vector.scalar_tensor_tensor(
+                out=result[:],
+                in0=bank[:, 0 : hi - lo],
+                scalar=coef[:, 4 + m : 5 + m],
+                in1=theta_sb[m // 2][:, m % 2, cols],
+                op0=MULT,
+                op1=ADD,
+            )
+            free_banks.append(b)
+            nc.sync.dma_start(out=out[m * P : (m + 1) * P, cols], in_=result[:])
+
+        def second_product(m, n, lo=0, hi=N_TILE):
+            held = take_bank()
+            for g in range(GROUPS):
+                second_pass(held[1], g, m, n, lo, hi)
+            return held
+
+        make_identity(nc, ident[:])
+        nc.vector.memset(vec_rows[:].bitcast(I32), 0)
+        nc.vector.memset(warm[:], 0.0)
+        nc.scalar.dma_start(out=vec_rows[0:4, :], in_=fitness.rearrange("(g p) -> g p", p=P))
+        nc.scalar.dma_start(out=vec_rows[4:12, :], in_=eta.rearrange("(j p) -> j p", p=P))
+        nc.scalar.activation(out=warm[:, 4:5], in_=warm[:, 0:1], func=COPY, scale=warm[:, 1:2])
+        for n in range(N_TILES):
+            nc.vector.memset(b_scales[n][:].bitcast(I32), 0)
+        nc.vector.tensor_copy(out=ident_bf[:], in_=ident[:])
+
+        load_z(0, 0, 2)
+        load_c(0)
+        load_z(0, 2, 4)
+        load_z(1, 0, 2)
+        load_z(1, 2, 4)
+        load_z(2, 0, 4)
+        load_c(1)
+        load_z(3, 0, 4)
+        load_b(0)
+        load_b(1)
+        load_c(2)
+        load_theta(0)
+        load_theta(1)
+        load_b(2)
+        load_theta(2)
+        load_theta(3)
+
+        copy_z(0, 0, transpose_z(0, 0), True)
+        vb, vec_bank = take_bank(BF16, P)
+        nc.tensor.transpose(vec_bank[:], vec_rows[:], ident_bf[:])
+        nc.scalar.copy(out=coef[:], in_=vec_bank[:, 0:16])
+        free_banks.append(vb)
+        group_c(0, 0, 256)
+        quantize_z(0, 0)
+        quantize_c(0, 256)
+        copy_z(0, 1, transpose_z(0, 1), True)
+        quantize_z(0, 1)
+        copy_z(1, 0, transpose_z(1, 0), True)
+        copy_z(1, 1, transpose_z(1, 1), False)
+        quantize_z(1, 0)
+        first_product(0, 0)
+        first_product(0, 1)
+        quantize_z(1, 1)
+        held = transpose_z(2, 0)
+        group_c(1, 256, 512)
+        copy_z(2, 0, held, False)
+        copy_z(2, 1, transpose_z(2, 1), True)
+        quantize_c(256, 512)
+        quantize_h(0, 0, 2)
+        quantize_z(2, 0)
+        first_product(1, 0)
+        first_product(1, 1)
+        quantize_z(2, 1)
+        copy_z(3, 0, transpose_z(3, 0), False)
+        copy_z(3, 1, transpose_z(3, 1), False)
+        first_product(0, 2)
+        first_product(0, 3)
+        quantize_h(1, 0, 2)
+        quantize_z(3, 0)
+        quantize_z(3, 1)
+        first_product(1, 2, False)
+        first_product(1, 3)
+        quantize_h(0, 2, 4)
+
+        acc = [take_bank() for m in range(4)]
+        for i, (g, m) in enumerate([(0, 0), (0, 1), (1, 0), (1, 1), (0, 2), (0, 3), (1, 2), (1, 3)]):
+            second_pass(acc[m][1], g, m, 0, 0, N_TILE)
+            first_product(2 + i // 4, i % 4, i != 2)
+            if i == 0:
+                quantize_h(1, 2, 4)
+            if i % 2 == 1:
+                quantize_h(2 + i // 4, i % 4 - 1, i % 4 + 1)
+            if i == 3:
+                group_c(2, 512, 768)
+            if i == 5:
+                quantize_c(512, 768)
+        for m in range(4):
+            second_pass(acc[m][1], 2, m, 0, 0, N_TILE)
+        group_c(2, 768, 1024)
+        for m in range(4):
+            second_pass(acc[m][1], 3, m, 0, 0, N_TILE)
+            finish(acc[m], m, 0, 0, N_TILE)
+            if m == 0:
+                quantize_c(768, 1024)
+
+        early = [(m, n) for n in (1, 2) for m in range(4)]
+        for i, (m, n) in enumerate(early):
+            pair, g = divmod(i, GROUPS)
+            first_product(g, 4 + 2 * pair)
+            first_product(g, 5 + 2 * pair)
+            held = second_product(m, n)
+            quantize_h(g, 4 + 2 * pair, 6 + 2 * pair)
+            finish(held, m, n, 0, N_TILE)
+
+        for m in range(4, M_TILES):
+            for n in range(N_TILES):
+                if (m, n) != (M_TILES - 1, N_TILES - 1):
+                    finish(second_product(m, n), m, n, 0, N_TILE)
+        for lo in range(0, N_TILE, P):
+            finish(second_product(M_TILES - 1, N_TILES - 1, lo, lo + P), M_TILES - 1, N_TILES - 1, lo, lo + P)

@@ -49,6 +49,9 @@ def tile_low_rank_es_update_s13_kernel(tc, z, c, fitness, right_words, right_sca
         vec_rows = sb("vec_rows", [P, P], BF16)
         coef = sb("coef", [P, 16], F32)
         warm = sb("warm", [P, 8], F32)
+        idle_in = sb("idle_in", [P, PACK * P], BF16)
+        idle_codes = sb("idle_codes", [P, P], U32)
+        idle_scales = sb("idle_scales", [P, P], U8)
 
         z_raw = [sb("z_raw%d" % g, [P, PACK, K], BF16) for g in range(GROUPS)]
         z_grp = [sb("z_grp%d" % g, [P, PACK, P, PACK], BF16) for g in range(GROUPS)]
@@ -194,19 +197,35 @@ def tile_low_rank_es_update_s13_kernel(tc, z, c, fitness, right_words, right_sca
                 second_pass(held[1], g, m, n, lo, hi)
             return held
 
+        def keep_busy(count):
+            b, bank = take_bank()
+            for i in range(count):
+                nc.tensor.matmul_mx(
+                    out=bank[:, (i % PACK) * P : (i % PACK + 1) * P],
+                    lhsT=idle_codes[:].bitcast(FP8X4),
+                    lhsT_scale=idle_scales[:],
+                    rhs=idle_codes[:].bitcast(FP8X4),
+                    rhs_scale=idle_scales[:],
+                    start=True,
+                    stop=True,
+                )
+            free_banks.append(b)
+
         make_identity(nc, ident[:])
+        nc.vector.memset(idle_in[:], 1.0)
         nc.vector.memset(vec_rows[:].bitcast(I32), 0)
         nc.vector.memset(warm[:], 0.0)
-        nc.scalar.dma_start(out=vec_rows[0:4, :], in_=fitness.rearrange("(g p) -> g p", p=P))
-        nc.scalar.dma_start(out=vec_rows[4:12, :], in_=eta.rearrange("(j p) -> j p", p=P))
-        nc.scalar.activation(out=warm[:, 4:5], in_=warm[:, 0:1], func=COPY, scale=warm[:, 1:2])
+        nc.vector.quantize_mx(out=idle_codes[:].bitcast(FP8X4), scales=idle_scales[:], in_=idle_in[:])
         for n in range(N_TILES):
             nc.vector.memset(b_scales[n][:].bitcast(I32), 0)
         nc.vector.tensor_copy(out=ident_bf[:], in_=ident[:])
 
         load_z(0, 0, 2)
-        load_c(0)
         load_z(0, 2, 4)
+        load_c(0)
+        nc.scalar.dma_start(out=vec_rows[0:4, :], in_=fitness.rearrange("(g p) -> g p", p=P))
+        nc.scalar.dma_start(out=vec_rows[4:12, :], in_=eta.rearrange("(j p) -> j p", p=P))
+        nc.scalar.activation(out=warm[:, 4:5], in_=warm[:, 0:1], func=COPY, scale=warm[:, 1:2])
         load_z(1, 0, 2)
         load_z(1, 2, 4)
         load_z(2, 0, 4)
@@ -221,16 +240,18 @@ def tile_low_rank_es_update_s13_kernel(tc, z, c, fitness, right_words, right_sca
         load_theta(2)
         load_theta(3)
 
+        keep_busy(11)
         copy_z(0, 0, transpose_z(0, 0), True)
+        copy_z(0, 1, transpose_z(0, 1), True)
         vb, vec_bank = take_bank(BF16, P)
         nc.tensor.transpose(vec_bank[:], vec_rows[:], ident_bf[:])
         nc.scalar.copy(out=coef[:], in_=vec_bank[:, 0:16])
         free_banks.append(vb)
-        group_c(0, 0, 256)
+        keep_busy(8)
         quantize_z(0, 0)
-        quantize_c(0, 256)
-        copy_z(0, 1, transpose_z(0, 1), True)
+        group_c(0, 0, 256)
         quantize_z(0, 1)
+        quantize_c(0, 256)
         copy_z(1, 0, transpose_z(1, 0), True)
         copy_z(1, 1, transpose_z(1, 1), False)
         quantize_z(1, 0)

@@ -229,24 +229,20 @@ def tile_low_rank_es_update_s13_kernel(tc, z, c, fitness, right_words, right_sca
         load_z(1, 0, 2)
         load_z(1, 2, 4)
         load_z(2, 0, 4)
-        load_c(1)
         load_z(3, 0, 4)
         load_b(0)
+        load_c(1)
         load_b(1)
-        load_c(2)
         load_theta(0)
-        load_theta(1)
         load_b(2)
+        load_c(2)
+        load_theta(1)
         load_theta(2)
         load_theta(3)
 
         keep_busy(11)
         copy_z(0, 0, transpose_z(0, 0), True)
         copy_z(0, 1, transpose_z(0, 1), True)
-        vb, vec_bank = take_bank(BF16, P)
-        nc.tensor.transpose(vec_bank[:], vec_rows[:], ident_bf[:])
-        nc.scalar.copy(out=coef[:], in_=vec_bank[:, 0:16])
-        free_banks.append(vb)
         keep_busy(8)
         quantize_z(0, 0)
         group_c(0, 0, 256)
@@ -254,64 +250,79 @@ def tile_low_rank_es_update_s13_kernel(tc, z, c, fitness, right_words, right_sca
         quantize_c(0, 256)
         copy_z(1, 0, transpose_z(1, 0), True)
         copy_z(1, 1, transpose_z(1, 1), False)
+        vb, vec_bank = take_bank(BF16, P)
+        nc.tensor.transpose(vec_bank[:], vec_rows[:], ident_bf[:])
+        nc.scalar.copy(out=coef[:], in_=vec_bank[:, 0:16])
+        free_banks.append(vb)
         quantize_z(1, 0)
-        first_product(0, 0)
-        first_product(0, 1)
-        quantize_z(1, 1)
-        held = transpose_z(2, 0)
-        group_c(1, 256, 512)
-        copy_z(2, 0, held, False)
-        copy_z(2, 1, transpose_z(2, 1), True)
-        quantize_c(256, 512)
-        quantize_h(0, 0, 2)
-        quantize_z(2, 0)
-        first_product(1, 0)
-        first_product(1, 1)
-        quantize_z(2, 1)
-        copy_z(3, 0, transpose_z(3, 0), False)
-        copy_z(3, 1, transpose_z(3, 1), False)
-        first_product(0, 2)
-        first_product(0, 3)
-        quantize_h(1, 0, 2)
-        quantize_z(3, 0)
+        for g in (0, 1):
+            first_product(g, 0)
+            first_product(g, 1)
+            quantize_z(g + 1, 1)
+            copy_z(g + 2, 0, transpose_z(g + 2, 0), False)
+            copy_z(g + 2, 1, transpose_z(g + 2, 1), True)
+            quantize_h(g, 0, 2)
+            quantize_z(g + 2, 0)
+        first_product(2, 0)
+        first_product(2, 1)
         quantize_z(3, 1)
-        first_product(1, 2, False)
-        first_product(1, 3)
+        group_c(1, 256, 512)
+        quantize_h(2, 0, 2)
+        quantize_c(256, 512)
+
+        def first_pair(g, pair):
+            first_product(g, 2 * pair)
+            first_product(g, 2 * pair + 1)
+
+        a0 = take_bank()
+        a1 = take_bank()
+        for g in (0, 1):
+            second_pass(a0[1], g, 0, 0, 0, N_TILE)
+            second_pass(a1[1], g, 1, 0, 0, N_TILE)
+        first_pair(3, 0)
+        quantize_h(3, 0, 2)
+        second_pass(a0[1], 2, 0, 0, 0, N_TILE)
+        second_pass(a1[1], 2, 1, 0, 0, N_TILE)
+        first_pair(0, 1)
+        a2 = take_bank()
+        second_pass(a2[1], 0, 0, 1, 0, N_TILE)
+        second_pass(a2[1], 1, 0, 1, 0, N_TILE)
+        second_pass(a0[1], 3, 0, 0, 0, N_TILE)
+        second_pass(a1[1], 3, 1, 0, 0, N_TILE)
         quantize_h(0, 2, 4)
+        first_pair(1, 1)
+        finish(a0, 0, 0, 0, N_TILE)
+        second_pass(a2[1], 2, 0, 1, 0, N_TILE)
+        second_pass(a2[1], 3, 0, 1, 0, N_TILE)
+        quantize_h(1, 2, 4)
+        finish(a1, 1, 0, 0, N_TILE)
+        first_pair(2, 1)
+        held = second_product(1, 1)
+        finish(a2, 0, 1, 0, N_TILE)
+        quantize_h(2, 2, 4)
+        first_pair(3, 1)
+        finish(held, 1, 1, 0, N_TILE)
+        held = second_product(0, 2)
+        quantize_h(3, 2, 4)
+        group_c(2, 512, 768)
+        finish(held, 0, 2, 0, N_TILE)
+        quantize_c(512, 768)
+        finish(second_product(1, 2), 1, 2, 0, N_TILE)
 
-        acc = [take_bank() for m in range(4)]
-        for i, (g, m) in enumerate([(0, 0), (0, 1), (1, 0), (1, 1), (0, 2), (0, 3), (1, 2), (1, 3)]):
-            second_pass(acc[m][1], g, m, 0, 0, N_TILE)
-            first_product(2 + i // 4, i % 4, i != 2)
-            if i == 0:
-                quantize_h(1, 2, 4)
-            if i % 2 == 1:
-                quantize_h(2 + i // 4, i % 4 - 1, i % 4 + 1)
-            if i == 3:
-                group_c(2, 512, 768)
-            if i == 5:
-                quantize_c(512, 768)
-        for m in range(4):
-            second_pass(acc[m][1], 2, m, 0, 0, N_TILE)
-        group_c(2, 768, 1024)
-        for m in range(4):
-            second_pass(acc[m][1], 3, m, 0, 0, N_TILE)
-            finish(acc[m], m, 0, 0, N_TILE)
-            if m == 0:
-                quantize_c(768, 1024)
-
-        early = [(m, n) for n in (1, 2) for m in range(4)]
-        for i, (m, n) in enumerate(early):
-            pair, g = divmod(i, GROUPS)
-            first_product(g, 4 + 2 * pair)
-            first_product(g, 5 + 2 * pair)
-            held = second_product(m, n)
-            quantize_h(g, 4 + 2 * pair, 6 + 2 * pair)
-            finish(held, m, n, 0, N_TILE)
-
-        for m in range(4, M_TILES):
-            for n in range(N_TILES):
-                if (m, n) != (M_TILES - 1, N_TILES - 1):
-                    finish(second_product(m, n), m, n, 0, N_TILE)
-        for lo in range(0, N_TILE, P):
-            finish(second_product(M_TILES - 1, N_TILES - 1, lo, lo + P), M_TILES - 1, N_TILES - 1, lo, lo + P)
+        for pair in range(1, 4):
+            tiles = [(2 * pair + h, n) for n in range(N_TILES) for h in range(2)]
+            for i, (m, n) in enumerate(tiles):
+                if (m, n) == (M_TILES - 1, N_TILES - 1):
+                    for lo in range(0, N_TILE, P):
+                        finish(second_product(m, n, lo, lo + P), m, n, lo, lo + P)
+                else:
+                    held = second_product(m, n)
+                    if pair < 3 and 1 <= i <= GROUPS:
+                        quantize_h(i - 1, 2 * pair + 2, 2 * pair + 4)
+                    if pair < 3 and i < GROUPS:
+                        first_pair(i, pair + 1)
+                    if pair == 1 and i == 4:
+                        group_c(2, 768, 1024)
+                    finish(held, m, n, 0, N_TILE)
+                    if pair == 1 and i == 4:
+                        quantize_c(768, 1024)

@@ -30,6 +30,7 @@ def tile_low_rank_es_update_s13_kernel(tc, z, c, fitness, right_words, right_sca
     nc = tc.nc
     with ExitStack() as ctx:
         keep = ctx.enter_context(tc.tile_pool(name="keep", bufs=1))
+        stage = ctx.enter_context(tc.tile_pool(name="stage", bufs=4))
         psum = ctx.enter_context(tc.psum_pool(name="psum", bufs=1))
         ctx.enter_context(tc.manual_schedule())
 
@@ -87,10 +88,9 @@ def tile_low_rank_es_update_s13_kernel(tc, z, c, fitness, right_words, right_sca
             words = right_words.bitcast(I32).rearrange("g p w -> p g w")
             nc.sync.dma_start(out=b_words[n][:].bitcast(I32), in_=words[:, :, n * 256 : (n + 1) * 256])
 
-        def load_theta(j):
-            nc.sync.dma_start(
-                out=theta_sb[j][:], in_=theta[j * 256 : (j + 1) * 256, :].rearrange("(a p) n -> p a n", p=P)
-            )
+        def load_theta(j, lo=0, hi=N):
+            rows = theta[j * 256 : (j + 1) * 256, :].rearrange("(a p) n -> p a n", p=P)
+            nc.sync.dma_start(out=theta_sb[j][:, :, lo:hi], in_=rows[:, :, lo:hi])
 
         def transpose_z(g, half):
             b, bank = take_bank()
@@ -119,12 +119,14 @@ def tile_low_rank_es_update_s13_kernel(tc, z, c, fitness, right_words, right_sca
                 in_=z_grp[g][:, 2 * half : 2 * half + 2, :, :].rearrange("p t r j -> p (t r j)"),
             )
 
-        def group_c(i, lo, hi):
+        def group_c(i, lo, hi, on_scalar=False):
             base = c_chunks[i][0]
-            nc.vector.tensor_copy(
-                out=c_grp[:, lo:hi, :].rearrange("p (c i) t -> p c t i", i=4),
-                in_=c_raw[i][:, :, lo - base : hi - base].rearrange("p t (c i) -> p c t i", i=4),
-            )
+            dst = c_grp[:, lo:hi, :].rearrange("p (c i) t -> p c t i", i=4)
+            src = c_raw[i][:, :, lo - base : hi - base].rearrange("p t (c i) -> p c t i", i=4)
+            if on_scalar:
+                nc.scalar.copy(out=dst, in_=src)
+            else:
+                nc.vector.tensor_copy(out=dst, in_=src)
 
         def quantize_c(lo, hi):
             nc.vector.quantize_mx(
@@ -233,9 +235,10 @@ def tile_low_rank_es_update_s13_kernel(tc, z, c, fitness, right_words, right_sca
         load_b(0)
         load_c(1)
         load_b(1)
-        load_theta(0)
-        load_b(2)
         load_c(2)
+        load_theta(0, 0, N_TILE)
+        load_b(2)
+        load_theta(0, N_TILE, N)
         load_theta(1)
         load_theta(2)
         load_theta(3)
@@ -270,44 +273,81 @@ def tile_low_rank_es_update_s13_kernel(tc, z, c, fitness, right_words, right_sca
         quantize_h(2, 0, 2)
         quantize_c(256, 512)
 
+        halves = {}
+
         def first_pair(g, pair):
-            first_product(g, 2 * pair)
-            first_product(g, 2 * pair + 1)
+            cols = slice(pair * 2 * P, (pair + 1) * 2 * P)
+            half = stage.tile([P, 2, 2 * P, 2], BF16, name="half", align_bytes=64)
+            for h in range(2):
+                b, bank = take_bank()
+                for tt in range(2):
+                    rows = slice((2 * h + tt) * P, (2 * h + tt + 1) * P)
+                    nc.tensor.matmul_mx(
+                        out=bank[:, tt * 2 * P : (tt + 1) * 2 * P],
+                        lhsT=z_codes[g][:, rows].bitcast(FP8X4),
+                        lhsT_scale=z_scales[g][:, rows],
+                        rhs=c_codes[:, cols].bitcast(FP8X4),
+                        rhs_scale=c_scales[:, cols],
+                        start=True,
+                        stop=True,
+                    )
+                nc.scalar.activation(
+                    out=half[:, h, :, :],
+                    in_=bank[:].rearrange("p (t w) -> p w t", t=2),
+                    func=COPY,
+                    scale=coef[:, g : g + 1],
+                )
+                free_banks.append(b)
+            halves[(g, pair)] = half
+
+        def join_pair(g, pair):
+            cols = slice(pair * 2 * P, (pair + 1) * 2 * P)
+            nc.vector.tensor_copy(
+                out=h_grp[g][:, cols, :].rearrange("p w (h t) -> p w h t", h=2),
+                in_=halves[(g, pair)][:].rearrange("p h w t -> p w h t"),
+            )
 
         a0 = take_bank()
         a1 = take_bank()
         for g in (0, 1):
             second_pass(a0[1], g, 0, 0, 0, N_TILE)
             second_pass(a1[1], g, 1, 0, 0, N_TILE)
-        first_pair(3, 0)
+        first_product(3, 0)
+        first_product(3, 1)
         quantize_h(3, 0, 2)
         second_pass(a0[1], 2, 0, 0, 0, N_TILE)
         second_pass(a1[1], 2, 1, 0, 0, N_TILE)
         first_pair(0, 1)
+        group_c(2, 512, 768)
         a2 = take_bank()
         second_pass(a2[1], 0, 0, 1, 0, N_TILE)
         second_pass(a2[1], 1, 0, 1, 0, N_TILE)
         second_pass(a0[1], 3, 0, 0, 0, N_TILE)
         second_pass(a1[1], 3, 1, 0, 0, N_TILE)
-        quantize_h(0, 2, 4)
+        join_pair(0, 1)
+        quantize_c(512, 768)
         first_pair(1, 1)
-        finish(a0, 0, 0, 0, N_TILE)
         second_pass(a2[1], 2, 0, 1, 0, N_TILE)
         second_pass(a2[1], 3, 0, 1, 0, N_TILE)
-        quantize_h(1, 2, 4)
-        finish(a1, 1, 0, 0, N_TILE)
+        quantize_h(0, 2, 4)
+        finish(a0, 0, 0, 0, N_TILE)
+        join_pair(1, 1)
         first_pair(2, 1)
-        held = second_product(1, 1)
-        finish(a2, 0, 1, 0, N_TILE)
+        a3 = second_product(1, 1)
+        finish(a1, 1, 0, 0, N_TILE)
+        join_pair(2, 1)
+        quantize_h(1, 2, 4)
         quantize_h(2, 2, 4)
         first_pair(3, 1)
-        finish(held, 1, 1, 0, N_TILE)
-        held = second_product(0, 2)
+        a4 = second_product(0, 2)
+        group_c(2, 768, 1024, True)
+        join_pair(3, 1)
+        finish(a2, 0, 1, 0, N_TILE)
         quantize_h(3, 2, 4)
-        group_c(2, 512, 768)
-        finish(held, 0, 2, 0, N_TILE)
-        quantize_c(512, 768)
-        finish(second_product(1, 2), 1, 2, 0, N_TILE)
+        a5 = second_product(1, 2)
+        finish(a3, 1, 1, 0, N_TILE)
+        finish(a4, 0, 2, 0, N_TILE)
+        finish(a5, 1, 2, 0, N_TILE)
 
         for pair in range(1, 4):
             tiles = [(2 * pair + h, n) for n in range(N_TILES) for h in range(2)]
@@ -317,12 +357,12 @@ def tile_low_rank_es_update_s13_kernel(tc, z, c, fitness, right_words, right_sca
                         finish(second_product(m, n, lo, lo + P), m, n, lo, lo + P)
                 else:
                     held = second_product(m, n)
-                    if pair < 3 and 1 <= i <= GROUPS:
-                        quantize_h(i - 1, 2 * pair + 2, 2 * pair + 4)
                     if pair < 3 and i < GROUPS:
                         first_pair(i, pair + 1)
-                    if pair == 1 and i == 4:
-                        group_c(2, 768, 1024)
+                    if pair < 3 and 1 <= i <= GROUPS:
+                        join_pair(i - 1, pair + 1)
                     finish(held, m, n, 0, N_TILE)
-                    if pair == 1 and i == 4:
+                    if pair < 3 and 1 <= i <= GROUPS:
+                        quantize_h(i - 1, 2 * pair + 2, 2 * pair + 4)
+                    if pair == 1 and i == 0:
                         quantize_c(768, 1024)

from contextlib import ExitStack

import concourse.mybir as mybir
from concourse.masks import make_identity

POP, K, M, N = 2048, 512, 1024, 1536
FLOPS = 2 * POP * K * M + 2 * POP * M * N

F32 = mybir.dt.float32
BF16 = mybir.dt.bfloat16
I32 = mybir.dt.int32
U32 = mybir.dt.uint32
U8 = mybir.dt.uint8
FP8X4 = mybir.dt.float8_e4m3fn_x4
FP4X4 = mybir.dt.float4_e2m1fn_x4
COPY = mybir.ActivationFunctionType.Copy
MULT = mybir.AluOpType.mult
ADD = mybir.AluOpType.add

P = 128
PACK = 4
GROUPS = POP // (P * PACK)
M_TILES = M // P
N_TILE = 512
N_TILES = N // N_TILE
BANKS = 8


def tile_low_rank_es_update_s13_kernel(tc, z, c, fitness, right_words, right_scales, eta, theta, out):
    nc = tc.nc
    with ExitStack() as ctx:
        keep = ctx.enter_context(tc.tile_pool(name="keep", bufs=1))
        stage = ctx.enter_context(tc.tile_pool(name="stage", bufs=4))
        psum = ctx.enter_context(tc.psum_pool(name="psum", bufs=1))
        ctx.enter_context(tc.manual_schedule())

        def sb(name, shape, dtype):
            return keep.tile(shape, dtype, name=name, align_bytes=64)

        free_banks = list(range(BANKS))

        def take_bank(dtype=F32, width=512):
            b = free_banks[0]
            free_banks.remove(b)
            t = psum.tile([P, width], dtype, name="bank%d" % b)
            return b, t

        ident = sb("ident", [P, P], F32)
        ident_bf = sb("ident_bf", [P, P], BF16)
        vec_rows = sb("vec_rows", [P, P], BF16)
        coef = sb("coef", [P, 16], F32)
        warm = sb("warm", [P, 8], F32)
        idle_in = sb("idle_in", [P, PACK * P], BF16)
        idle_codes = sb("idle_codes", [P, P], U32)
        idle_scales = sb("idle_scales", [P, P], U8)

        z_raw = [sb("z_raw%d" % g, [P, PACK, K], BF16) for g in range(GROUPS)]
        z_grp = [sb("z_grp%d" % g, [P, PACK, P, PACK], BF16) for g in range(GROUPS)]
        z_codes = [sb("z_codes%d" % g, [P, PACK * P], U32) for g in range(GROUPS)]
        z_scales = [sb("z_scales%d" % g, [P, PACK * P], U8) for g in range(GROUPS)]
        c_chunks = [(0, 256), (256, 512), (512, 1024)]
        c_raw = [sb("c_raw%d" % i, [P, PACK, hi - lo], BF16) for i, (lo, hi) in enumerate(c_chunks)]
        c_grp = sb("c_grp", [P, M, PACK], BF16)
        c_codes = sb("c_codes", [P, M], U32)
        c_scales = sb("c_scales", [P, M], U8)
        h_grp = [sb("h_grp%d" % g, [P, M, PACK], BF16) for g in range(GROUPS)]
        h_codes = [sb("h_codes%d" % g, [P, M], U32) for g in range(GROUPS)]
        h_scales = [sb("h_scales%d" % g, [P, M], U8) for g in range(GROUPS)]
        b_words = [sb("b_words%d" % n, [P, GROUPS, 2 * N_TILE], U8) for n in range(N_TILES)]
        b_scales = [sb("b_scales%d" % n, [P, GROUPS, N_TILE], U8) for n in range(N_TILES)]
        theta_sb = [sb("theta%d" % j, [P, 2, N], BF16) for j in range(M_TILES // 2)]

        def load_z(g, t0, t1):
            rows = z[g * 512 : (g + 1) * 512, :].rearrange("(p t) k -> p t k", t=PACK)
            nc.sync.dma_start(out=z_raw[g][:, t0:t1, :], in_=rows[:, t0:t1, :])

        def load_c(i):
            lo, hi = c_chunks[i]
            nc.sync.dma_start(out=c_raw[i][:], in_=c.rearrange("(p j) w -> p j w", j=PACK)[:, :, lo:hi])

        def load_b(n):
            rows = right_scales.bitcast(I32).rearrange("g (q r) w -> r q g w", r=4)
            for r in range(4):
                nc.sync.dma_start(
                    out=b_scales[n][:].bitcast(I32)[r:P:32, :, :],
                    in_=rows[r, :, :, n * 128 : (n + 1) * 128],
                )
            words = right_words.bitcast(I32).rearrange("g p w -> p g w")
            nc.sync.dma_start(out=b_words[n][:].bitcast(I32), in_=words[:, :, n * 256 : (n + 1) * 256])

        def load_theta(j, lo=0, hi=N):
            rows = theta[j * 256 : (j + 1) * 256, :].rearrange("(a p) n -> p a n", p=P)
            nc.sync.dma_start(out=theta_sb[j][:, :, lo:hi], in_=rows[:, :, lo:hi])

        def transpose_z(g, half):
            b, bank = take_bank()
            for tt in range(2):
                words = z_raw[g][:, 2 * half + tt, :].bitcast(F32)
                for u in range(2):
                    col = (2 * tt + u) * P
                    nc.tensor.transpose(bank[:, col : col + P], words[:, u : 2 * P : 2], ident[:])
            return b, bank

        def copy_z(g, half, held, on_scalar):
            b, bank = held
            dst = z_grp[g][:, 2 * half : 2 * half + 2, :, :].bitcast(F32)
            src = bank[:].rearrange("p (t u r) -> p t r u", t=2, u=2)
            if on_scalar:
                nc.scalar.copy(out=dst, in_=src)
            else:
                nc.vector.tensor_copy(out=dst, in_=src)
            free_banks.append(b)

        def quantize_z(g, half):
            cols = slice(half * 256, (half + 1) * 256)
            nc.vector.quantize_mx(
                out=z_codes[g][:, cols].bitcast(FP8X4),
                scales=z_scales[g][:, cols],
                in_=z_grp[g][:, 2 * half : 2 * half + 2, :, :].rearrange("p t r j -> p (t r j)"),
            )

        def group_c(i, lo, hi, on_scalar=False):
            base = c_chunks[i][0]
            dst = c_grp[:, lo:hi, :].rearrange("p (c i) t -> p c t i", i=4)
            src = c_raw[i][:, :, lo - base : hi - base].rearrange("p t (c i) -> p c t i", i=4)
            if on_scalar:
                nc.scalar.copy(out=dst, in_=src)
            else:
                nc.vector.tensor_copy(out=dst, in_=src)

        def quantize_c(lo, hi):
            nc.vector.quantize_mx(
                out=c_codes[:, lo:hi].bitcast(FP8X4),
                scales=c_scales[:, lo:hi],
                in_=c_grp[:, lo:hi, :].rearrange("p w j -> p (w j)"),
            )

        def first_product(g, m, on_scalar=True):
            b, bank = take_bank()
            cols = slice(m * P, (m + 1) * P)
            for t in range(PACK):
                rows = slice(t * P, (t + 1) * P)
                nc.tensor.matmul_mx(
                    out=bank[:, rows],
                    lhsT=z_codes[g][:, rows].bitcast(FP8X4),
                    lhsT_scale=z_scales[g][:, rows],
                    rhs=c_codes[:, cols].bitcast(FP8X4),
                    rhs_scale=c_scales[:, cols],
                    start=True,
                    stop=True,
                )
            src = bank[:].rearrange("p (t w) -> p w t", t=PACK)
            if on_scalar:
                nc.scalar.activation(out=h_grp[g][:, cols, :], in_=src, func=COPY, scale=coef[:, g : g + 1])
            else:
                nc.vector.tensor_scalar(
                    out=h_grp[g][:, cols, :], in0=src, scalar1=coef[:, g : g + 1], scalar2=None, op0=MULT
                )
            free_banks.append(b)

        def quantize_h(g, m0, m1):
            cols = slice(m0 * P, m1 * P)
            nc.vector.quantize_mx(
                out=h_codes[g][:, cols].bitcast(FP8X4),
                scales=h_scales[g][:, cols],
                in_=h_grp[g][:, cols, :].rearrange("p w j -> p (w j)"),
            )

        def second_pass(bank, g, m, n, lo, hi):
            cols = slice(m * P, (m + 1) * P)
            nc.tensor.matmul_mx(
                out=bank[:, 0 : hi - lo],
                lhsT=h_codes[g][:, cols].bitcast(FP8X4),
                lhsT_scale=h_scales[g][:, cols],
                rhs=b_words[n][:, g, 2 * lo : 2 * hi].bitcast(FP4X4),
                rhs_scale=b_scales[n][:, g, lo:hi],
                start=(g == 0),
                stop=(g == GROUPS - 1),
            )

        def finish(held, m, n, lo, hi):
            b, bank = held
            result = sb("result_%d_%d_%d" % (m, n, lo), [P, hi - lo], F32)
            cols = slice(n * N_TILE + lo, n * N_TILE + hi)
            nc.vector.scalar_tensor_tensor(
                out=result[:],
                in0=bank[:, 0 : hi - lo],
                scalar=coef[:, 4 + m : 5 + m],
                in1=theta_sb[m // 2][:, m % 2, cols],
                op0=MULT,
                op1=ADD,
            )
            free_banks.append(b)
            nc.sync.dma_start(out=out[m * P : (m + 1) * P, cols], in_=result[:])

        def second_product(m, n, lo=0, hi=N_TILE):
            held = take_bank()
            for g in range(GROUPS):
                second_pass(held[1], g, m, n, lo, hi)
            return held

        def keep_busy(count):
            b, bank = take_bank()
            for i in range(count):
                nc.tensor.matmul_mx(
                    out=bank[:, (i % PACK) * P : (i % PACK + 1) * P],
                    lhsT=idle_codes[:].bitcast(FP8X4),
                    lhsT_scale=idle_scales[:],
                    rhs=idle_codes[:].bitcast(FP8X4),
                    rhs_scale=idle_scales[:],
                    start=True,
                    stop=True,
                )
            free_banks.append(b)

        make_identity(nc, ident[:])
        nc.vector.memset(idle_in[:], 1.0)
        nc.vector.memset(vec_rows[:].bitcast(I32), 0)
        nc.vector.memset(warm[:], 0.0)
        nc.vector.quantize_mx(out=idle_codes[:].bitcast(FP8X4), scales=idle_scales[:], in_=idle_in[:])
        for n in range(N_TILES):
            nc.vector.memset(b_scales[n][:].bitcast(I32), 0)
        nc.vector.tensor_copy(out=ident_bf[:], in_=ident[:])

        load_z(0, 0, 2)
        load_z(0, 2, 4)
        load_c(0)
        nc.scalar.dma_start(out=vec_rows[0:4, :], in_=fitness.rearrange("(g p) -> g p", p=P))
        nc.scalar.dma_start(out=vec_rows[4:12, :], in_=eta.rearrange("(j p) -> j p", p=P))
        nc.scalar.activation(out=warm[:, 4:5], in_=warm[:, 0:1], func=COPY, scale=warm[:, 1:2])
        load_z(1, 0, 2)
        load_z(1, 2, 4)
        load_z(2, 0, 4)
        load_z(3, 0, 4)
        load_b(0)
        load_c(1)
        load_b(1)
        load_c(2)
        load_theta(0, 0, N_TILE)
        load_b(2)
        load_theta(0, N_TILE, N)
        load_theta(1)
        load_theta(2)
        load_theta(3)

        keep_busy(11)
        copy_z(0, 0, transpose_z(0, 0), True)
        copy_z(0, 1, transpose_z(0, 1), True)
        keep_busy(8)
        quantize_z(0, 0)
        group_c(0, 0, 256)
        quantize_z(0, 1)
        quantize_c(0, 256)
        copy_z(1, 0, transpose_z(1, 0), True)
        copy_z(1, 1, transpose_z(1, 1), False)
        vb, vec_bank = take_bank(BF16, P)
        nc.tensor.transpose(vec_bank[:], vec_rows[:], ident_bf[:])
        nc.scalar.copy(out=coef[:], in_=vec_bank[:, 0:16])
        free_banks.append(vb)
        quantize_z(1, 0)
        for g in (0, 1):
            first_product(g, 0)
            first_product(g, 1)
            quantize_z(g + 1, 1)
            copy_z(g + 2, 0, transpose_z(g + 2, 0), False)
            copy_z(g + 2, 1, transpose_z(g + 2, 1), True)
            quantize_h(g, 0, 2)
            quantize_z(g + 2, 0)
        first_product(2, 0)
        first_product(2, 1)
        quantize_z(3, 1)
        group_c(1, 256, 512)
        quantize_h(2, 0, 2)
        quantize_c(256, 512)

        halves = {}

        def first_pair(g, pair):
            cols = slice(pair * 2 * P, (pair + 1) * 2 * P)
            half = stage.tile([P, 2, 2 * P, 2], BF16, name="half", align_bytes=64)
            for h in range(2):
                b, bank = take_bank()
                for tt in range(2):
                    rows = slice((2 * h + tt) * P, (2 * h + tt + 1) * P)
                    nc.tensor.matmul_mx(
                        out=bank[:, tt * 2 * P : (tt + 1) * 2 * P],
                        lhsT=z_codes[g][:, rows].bitcast(FP8X4),
                        lhsT_scale=z_scales[g][:, rows],
                        rhs=c_codes[:, cols].bitcast(FP8X4),
                        rhs_scale=c_scales[:, cols],
                        start=True,
                        stop=True,
                    )
                nc.scalar.activation(
                    out=half[:, h, :, :],
                    in_=bank[:].rearrange("p (t w) -> p w t", t=2),
                    func=COPY,
                    scale=coef[:, g : g + 1],
                )
                free_banks.append(b)
            halves[(g, pair)] = half

        def join_pair(g, pair):
            cols = slice(pair * 2 * P, (pair + 1) * 2 * P)
            nc.vector.tensor_copy(
                out=h_grp[g][:, cols, :].rearrange("p w (h t) -> p w h t", h=2),
                in_=halves[(g, pair)][:].rearrange("p h w t -> p w h t"),
            )

        a0 = take_bank()
        a1 = take_bank()
        for g in (0, 1):
            second_pass(a0[1], g, 0, 0, 0, N_TILE)
            second_pass(a1[1], g, 1, 0, 0, N_TILE)
        first_product(3, 0)
        first_product(3, 1)
        quantize_h(3, 0, 2)
        second_pass(a0[1], 2, 0, 0, 0, N_TILE)
        second_pass(a1[1], 2, 1, 0, 0, N_TILE)
        first_pair(0, 1)
        group_c(2, 512, 768)
        a2 = take_bank()
        second_pass(a2[1], 0, 0, 1, 0, N_TILE)
        second_pass(a2[1], 1, 0, 1, 0, N_TILE)
        second_pass(a0[1], 3, 0, 0, 0, N_TILE)
        second_pass(a1[1], 3, 1, 0, 0, N_TILE)
        join_pair(0, 1)
        quantize_c(512, 768)
        first_pair(1, 1)
        second_pass(a2[1], 2, 0, 1, 0, N_TILE)
        second_pass(a2[1], 3, 0, 1, 0, N_TILE)
        quantize_h(0, 2, 4)
        finish(a0, 0, 0, 0, N_TILE)
        join_pair(1, 1)
        first_pair(2, 1)
        a3 = second_product(1, 1)
        finish(a1, 1, 0, 0, N_TILE)
        join_pair(2, 1)
        quantize_h(1, 2, 4)
        quantize_h(2, 2, 4)
        first_pair(3, 1)
        a4 = second_product(0, 2)
        group_c(2, 768, 1024, True)
        join_pair(3, 1)
        finish(a2, 0, 1, 0, N_TILE)
        quantize_h(3, 2, 4)
        a5 = second_product(1, 2)
        finish(a3, 1, 1, 0, N_TILE)
        finish(a4, 0, 2, 0, N_TILE)
        finish(a5, 1, 2, 0, N_TILE)

        for pair in range(1, 4):
            tiles = [(2 * pair + h, n) for n in range(N_TILES) for h in range(2)]
            for i, (m, n) in enumerate(tiles):
                if (m, n) == (M_TILES - 1, N_TILES - 1):
                    for lo in range(0, N_TILE, P):
                        finish(second_product(m, n, lo, lo + P), m, n, lo, lo + P)
                else:
                    held = second_product(m, n)
                    if pair < 3 and i < GROUPS:
                        first_pair(i, pair + 1)
                    if pair < 3 and 1 <= i <= GROUPS:
                        join_pair(i - 1, pair + 1)
                    finish(held, m, n, 0, N_TILE)
                    if pair < 3 and 1 <= i <= GROUPS:
                        quantize_h(i - 1, 2 * pair + 2, 2 * pair + 4)
                    if pair == 1 and i == 0:
                        quantize_c(768, 1024)
